import numpy as np, ml_dtypes
CORES = [12,28,60,100,156,228]
N = 6
import mx_ref
NC = 512
BF = ml_dtypes.bfloat16
def setup_inputs(rng):
    def f(*shape):
        return mx_ref.flush((rng.standard_normal(shape, dtype=np.float32) * np.exp2(rng.integers(-2, 3, shape[:-1] + (1,)))).astype(BF))
    return {"x": f(N, 128, 512), "rt": f(N, 128, 512), "w": f(N, 128, 4 * NC)}
def setup_inputs_blocks(rng):
    d = setup_inputs(rng)
    for k in ("x", "rt", "w"): d[k] = mx_ref.spread(d[k], rng, 4)
    return d
def setup_inputs_wide(rng):
    d = setup_inputs(rng)
    for k in ("x", "rt", "w"): d[k] = mx_ref.flush((d[k].astype(np.float32) * np.exp2(rng.integers(-6, 7, (N, 1, 1))).astype(np.float32)).astype(BF))
    return d
def setup_inputs_near(rng):
    d = setup_inputs(rng); v = d["rt"].astype(np.float32).reshape(N, 128, -1, 4)
    d["rt"] = mx_ref.flush((v[:, :, :1] + v / 64).reshape(d["rt"].shape).astype(BF))
    return d
def setup_inputs_twins(rng):
    d = setup_inputs(rng); v = d["rt"].reshape(N, 128, -1, 4).copy()
    v[:, :, 1] = v[:, :, 0]
    d["rt"] = v.reshape(d["rt"].shape)
    return d
def reference(x, rt, w):
    W = [mx_ref.quantize(w[e]) for e in range(N)]
    y = np.zeros((N, 128, NC), np.float32)
    for j in range(N):
        X = mx_ref.quantize(x[j])
        lg = mx_ref.matmul(X, mx_ref.quantize(rt[j]))[:, :N]
        m = lg.max(axis=1, keepdims=True)
        for e in range(N):
            y[j] = y[j] + (lg[:, e:e + 1] == m) * (mx_ref.matmul(X, W[e]) * m)
    return {"y": y}

from concourse.bass import DstId, RemoteDMATransfer
from concourse.mybir import dt, AluOpType, AxisListType, ActivationFunctionType

N = 6
NC = 512
NSIM = 256
CUTS = (0, 176, 352, 512)
NCH = len(CUTS) - 1
HAND = (0, 1, 3, 2)
BLOCKS = (0, 1, 2)
SPLIT = True
DIRECT = True
OFF_N = 8
ON_N = 16
FUSE = False
VIA_MATE = ()
NBANK = 7
PIECES = [("c", CUTS[i], CUTS[i + 1]) for i in range(NCH)] + [("p", 0, NC)]
NUNIT = 2 + (N - 1) * NCH

SCRATCH = {
    "wb": ("sbuf", [128, 4 * NC], "bfloat16"),
    "xb": ("sbuf", [128, 512], "bfloat16"),
    "rb": ("sbuf", [128, 512], "bfloat16"),
    "xc": ("sbuf", [128, 128], "float8_e4m3fn_x4"),
    "xp": ("sbuf", [128, 128], "uint8"),
    "rc": ("sbuf", [128, 128], "float8_e4m3fn_x4"),
    "rp": ("sbuf", [128, 128], "uint8"),
    "wc": ("sbuf", [128, N * NC], "float8_e4m3fn_x4"),
    "wp": ("sbuf", [128, N * NC], "uint8"),
    "pl": ("psum", [128, 512], "float32"),
    "pw": ("psum", [128, NBANK * 512], "float32"),
    "m": ("sbuf", [128, 4], "float32"),
    "s": ("sbuf", [128, 8], "float32"),
    "t": ("sbuf", [128, N * NC], "float32"),
    "acc": ("sbuf", [128, NC], "float32"),
}
SEMAPHORES = (["lw%d" % i for i in range(NCH)] + ["qw%d" % i for i in range(NCH)] + ["lx", "lr", "qx", "qr", "pl", "sm", "ss"]
              + ["a%d_%d" % (e, i) for e in range(N) for i in range(NCH + 1)]
              + ["pm%d" % u for u in range(NUNIT)] + ["rd%d" % u for u in range(NUNIT)] + ["ad%d" % u for u in range(NUNIT)]
              + ["st%d" % i for i in range(NCH)] + ["dsent", "sent"])

_CACHE = {}


def _perms(items):
    if len(items) <= 1:
        return [list(items)]
    out = []
    for i in range(len(items)):
        for p in _perms(items[:i] + items[i + 1:]):
            out.append([items[i]] + p)
    return out


def _turns(dests):
    taken = [set() for _ in dests[0]]
    order = []

    def rec(s):
        if s == len(dests):
            return True
        for p in _perms(dests[s]):
            if all(p[k] not in taken[k] for k in range(len(p))):
                for k in range(len(p)):
                    taken[k].add(p[k])
                order.append(p)
                if rec(s + 1):
                    return True
                order.pop()
                for k in range(len(p)):
                    taken[k].discard(p[k])
        return False

    rec(0)
    return order


def _on_chip(topo, a, b):
    return topo.host(a) == topo.host(b) and topo.chip(a) == topo.chip(b)


def _plan(T, topo):
    if "plan" in _CACHE:
        return _CACHE["plan"]
    ranks = [int(c) for c in T.cores]
    helpers, direct, dests = [], [], []
    for s in range(N):
        home = ranks[s]
        others = [d for d in range(N) if d != s]
        near = [d for d in others if topo.may_write(home, ranks[d])]
        port = [c for c in range(NSIM) if c != home and _on_chip(topo, c, home)
                and all(topo.may_write(c, ranks[d]) for d in others)]
        far_die = [c for c in port if topo.die(c) != topo.die(home)]
        own_die = [c for c in port if topo.die(c) == topo.die(home)]
        helpers.append(far_die[:2] + own_die[:2])
        group = sorted(near + [s])
        direct.append(group[(group.index(s) + 1) % len(group)] if DIRECT else None)
        dests.append([d for d in others if d != direct[s]])
    order = _turns(dests)
    relay = {}
    for (s, d) in VIA_MATE:
        own = [c for c in range(NSIM) if topo.mates(c, ranks[d]) and topo.may_write(c, ranks[d])]
        seen = {}
        for i in range(len(PIECES)):
            die = topo.die(helpers[s][i])
            k = seen.get(die, 0)
            seen[die] = k + 1
            relay[(s, d, i)] = [c for c in own if topo.die(c) == die][k]
    p = {"ranks": ranks, "helpers": helpers, "direct": direct, "order": order, "relay": relay}
    _CACHE["plan"] = p
    return p


def _engines(mask, n):
    bits = [b for b in range(mask.bit_length()) if (mask >> b) & 1]
    out = 0
    for b in bits[:n]:
        out |= 1 << b
    return out


def _view(T, s, piece):
    kind, a, b = piece
    if kind == "c":
        return T.wc[:, s * NC + a:s * NC + b].bitcast(dt.uint8)
    return T.wp[:, s * NC + a:s * NC + b]


def _send(g, T, topo, src, dst, s, piece, rsem, n, lsem):
    rid, pid = topo.addr(dst, src)
    g.remote_dma(out_ap=_view(T, s, piece), in_ap=_view(T, s, piece), remote_sem=rsem, local_sem=lsem,
                 pid=pid, routing_id=rid, dma_engine_mask=_engines(topo.mask(src, dst), n))


def _send_many(g, T, topo, src, dsts, s, piece, rsem, n, lsem):
    if not FUSE or len(dsts) < 2:
        for d in dsts:
            _send(g, T, topo, src, d, s, piece, rsem, n, lsem)
        return n * len(dsts)
    mask = _engines(topo.mask(src, dsts[0]), n)
    ids = []
    for d in dsts:
        rid, pid = topo.addr(d, src)
        ids.append(DstId(rid=rid, pnc=pid))
    g.remote_dma_fused([RemoteDMATransfer(dst_ids=ids, dma_engine_mask=mask, remote_sem=rsem,
                                          srcs=[_view(T, s, piece)], dsts=[_view(T, s, piece) for _ in dsts])], local_sem=lsem)
    return n


def _helper_program(g, core, T, topo, P):
    ranks = P["ranks"]
    sent = 0
    for s in range(N):
        if core in P["helpers"][s]:
            i = P["helpers"][s].index(core)
            arr = T.sem["a%d_%d" % (s, i)]
            g.wait_ge(arr, ON_N)
            dsts = [P["relay"].get((s, d, i), ranks[d]) for d in P["order"][s]]
            sent += _send_many(g, T, topo, core, dsts, s, PIECES[i], arr, OFF_N, T.sem.sent)
    jobs = sorted((P["order"][s].index(d), s, d, i) for (s, d, i), c in P["relay"].items() if c == core)
    for _, s, d, i in jobs:
        arr = T.sem["a%d_%d" % (s, i)]
        g.wait_ge(arr, OFF_N)
        _send(g, T, topo, core, ranks[d], s, PIECES[i], arr, OFF_N, T.sem.sent)
        sent += OFF_N
    if sent:
        g.wait_ge(T.sem.sent, sent)


def rank_program(g, core, T, topo):
    P = _plan(T, topo)
    me = T.rank_of(core)
    if me is None:
        _helper_program(g, core, T, topo, P)
        return
    ranks, sem = P["ranks"], T.sem
    base = me * NC
    loaders = [g.sync, g.scalar]

    for i in range(NCH):
        a, b = 4 * CUTS[i], 4 * CUTS[i + 1]
        loaders[i % 2].dma_start(T.wb[:, a:b], T.w[:, a:b]).then_inc(sem["lw%d" % i], 16)
    loaders[NCH % 2].dma_start(T.xb[:], T.x[:]).then_inc(sem.lx, 16)
    loaders[(NCH + 1) % 2].dma_start(T.rb[:], T.rt[:]).then_inc(sem.lr, 16)

    for i in range(NCH):
        a, b = CUTS[i], CUTS[i + 1]
        g.vector.wait_ge(sem["lw%d" % i], 16)
        g.vector.quantize_mx(T.wc[:, base + a:base + b], T.wp[:, base + a:base + b], T.wb[:, 4 * a:4 * b]).then_inc(sem["qw%d" % i], 1)
    g.vector.wait_ge(sem.lx, 16)
    g.vector.quantize_mx(T.xc[:], T.xp[:], T.xb[:]).then_inc(sem.qx, 1)
    g.vector.wait_ge(sem.lr, 16)
    g.vector.quantize_mx(T.rc[:], T.rp[:], T.rb[:]).then_inc(sem.qr, 1)

    ready = 0
    for i in HAND:
        while ready < min(i + 1, NCH):
            g.wait_ge(sem["qw%d" % ready], 1)
            ready += 1
        _send(g, T, topo, core, P["helpers"][me][i], me, PIECES[i], sem["a%d_%d" % (me, i)], ON_N, sem.dsent)
    if P["direct"][me] is not None:
        d = ranks[P["direct"][me]]
        _send(g, T, topo, core, d, me, ("c", 0, NC), sem["a%d_0" % me], OFF_N, sem.sent)
        _send(g, T, topo, core, d, me, ("p", 0, NC), sem["a%d_0" % me], OFF_N, sem.sent)
        g.wait_ge(sem.sent, 2 * OFF_N)
    g.wait_ge(sem.dsent, ON_N * len(PIECES))

    units = [(me, 0, NC, [("qw%d" % i, 1) for i in range(NCH)])]
    for s in range(N):
        if P["direct"][s] == me:
            units.append((s, 0, NC, [("a%d_0" % s, 2 * OFF_N)]))
    last = {}
    for k in range(len(P["order"][0])):
        for s in range(N):
            if P["order"][s][k] == me:
                if SPLIT:
                    for i in BLOCKS:
                        last[i] = len(units)
                        units.append((s, CUTS[i], CUTS[i + 1], [("a%d_%d" % (s, NCH), OFF_N), ("a%d_%d" % (s, i), OFF_N)]))
                else:
                    last = {0: len(units)}
                    units.append((s, 0, NC, [("a%d_%d" % (s, i), OFF_N) for i in range(NCH + 1)]))

    g.tensor.wait_ge(sem.qx, 1)
    g.tensor.wait_ge(sem.qr, 1)
    g.tensor.matmul_mx(T.pl[:, 0:128], T.xc[:], T.xp[:], T.rc[:], T.rp[:], True, True).then_inc(sem.pl, 1)
    for u, (e, a, b, needs) in enumerate(units):
        for name, count in needs:
            g.tensor.wait_ge(sem[name], count)
        if u >= NBANK:
            g.tensor.wait_ge(sem["rd%d" % (u - NBANK)], 1)
        k = (u % NBANK) * 512
        g.tensor.matmul_mx(T.pw[:, k:k + b - a], T.xc[:], T.xp[:], T.wc[:, e * NC + a:e * NC + b],
                           T.wp[:, e * NC + a:e * NC + b], True, True).then_inc(sem["pm%d" % u], 1)

    g.vector.wait_ge(sem.pl, 1)
    g.vector.tensor_reduce(T.m[:, 0:1], T.pl[:, 0:N], AxisListType.X, AluOpType.max).then_inc(sem.sm, 1)
    g.vector.wait_ge(sem.sm, 1)
    g.vector.tensor_scalar(T.s[:, 0:N], T.pl[:, 0:N], T.m[:, 0:1], T.m[:, 0:1], AluOpType.is_equal, AluOpType.mult).then_inc(sem.ss, 1)
    g.vector.wait_ge(sem.ss, 1)
    g.scalar.wait_ge(sem.ss, 1)

    for u, (e, a, b, _) in enumerate(units):
        k = (u % NBANK) * 512
        pe = T.pw[:, k:k + b - a]
        if u == 0:
            g.vector.wait_ge(sem.pm0, 1)
            g.vector.tensor_scalar(T.acc[:], pe, T.s[:, e:e + 1], 0.0, AluOpType.mult, AluOpType.add).then_inc(sem.rd0, 1)
            g.vector.wait_ge(sem.rd0, 1)
            continue
        te = T.t[:, e * NC + a:e * NC + b]
        g.scalar.wait_ge(sem["pm%d" % u], 1)
        g.scalar.activation(te, pe, ActivationFunctionType.Identity, scale=T.s[:, e:e + 1]).then_inc(sem["rd%d" % u], 1)
        g.vector.wait_ge(sem["rd%d" % u], 1)
        if u > 1:
            g.vector.wait_ge(sem["ad%d" % (u - 1)], 1)
        g.vector.tensor_tensor(T.acc[:, a:b], T.acc[:, a:b], te, AluOpType.add).then_inc(sem["ad%d" % u], 1)

    done = sorted((u, i) for i, u in last.items())
    for u, i in done:
        a, b = units[u][1], units[u][2]
        g.sync.wait_ge(sem["ad%d" % u], 1)
        g.sync.dma_start(T.y[:, a:b], T.acc[:, a:b]).then_inc(sem["st%d" % i], 16)
    for u, i in done:
        g.sync.wait_ge(sem["st%d" % i], 16)
